import numpy as np
import ml_dtypes


def mxq(x, axis, fmt="e4m3"):
    dtype, down = {"e4m3": (ml_dtypes.float8_e4m3fn, 7), "e5m2": (ml_dtypes.float8_e5m2, 14)}[fmt]
    v = np.moveaxis(np.asarray(x, np.float32).astype(ml_dtypes.bfloat16).astype(np.float64), axis, -1)
    blocks = v.reshape(v.shape[:-1] + (-1, 32))
    amax = np.abs(blocks).max(-1, keepdims=True)
    byte = np.maximum(np.where(amax > 0, np.frexp(amax)[1] - 1 + 127, 0) - down, 1)
    scale = np.exp2(byte - 127.0)
    codes = (blocks / scale).astype(np.float32).astype(dtype).astype(np.float64)
    return np.moveaxis((codes * scale).reshape(v.shape), -1, axis)


WIDE = False


def mx_kscale(k):
    if not WIDE:
        return np.ones(k)
    levels = np.array([10, -10, 5, -5, 0])
    if k % 512:
        return np.exp2(np.random.permutation(np.resize(levels, k // 32))).repeat(32)
    a = np.empty((k // 512, 16))
    for p in range(k // 512):
        a[p, :8] = np.random.permutation(np.resize(levels, 8))
        for g in range(8):
            far = levels[np.abs(levels - a[p, g]) >= 10]
            a[p, g + 8] = far[np.random.randint(len(far))]
    return np.exp2(a.ravel()).repeat(32)


def f64(x):
    return np.asarray(x).astype(np.float64)


def striped(idx):
    return np.tile(idx.reshape(-1, 16).T, (8, 1)).astype(np.uint16)


def unstriped(offs):
    return offs[:16].T.reshape(-1).astype(np.int64)

def planes(y):
    n, m = y.shape
    v = y.astype(np.float32).astype(ml_dtypes.bfloat16).astype(np.float64).reshape(n // 32, 32, m)
    top = np.abs(v).max(1)
    byte = np.clip(np.where(top > 0, np.frexp(top)[1] - 1 + 127 - 7, 1), 1, 254)
    codes = (v * np.exp2(127.0 - byte)[:, None, :]).reshape(n, m).astype(np.float32).astype(ml_dtypes.float8_e4m3fn).view(np.uint8)
    words = codes.reshape(n // 512, 128, 4, m).transpose(0, 1, 3, 2)
    return np.ascontiguousarray(words), np.ascontiguousarray(byte.astype(np.uint8).reshape(n // 512, 16, m))


K, T, S, D, V, N = 512, 1024, 512, 3, 256, 512
P = 2 ** 7


def setup_inputs():
    n = np.random.standard_normal
    s = mx_kscale(K)[:, None]
    return {
        "xT": (n((K, T)) * s).astype(np.float32),
        "w1": (n((K, N)) / np.sqrt(K) / s).astype(np.float32),
        "score": np.tile(np.random.standard_normal((D, 1, V)), (1, P, 1)).astype(np.float32),
        "offs": striped(np.random.permutation(T)[:S]),
        "pos1": striped(np.random.permutation(S)[:V]),
        "pos2": striped(np.random.permutation(S)[:V]),
        "pos3": striped(np.random.permutation(S)[:V]),
    }


def reference(xT, w1, score, offs, pos1, pos2, pos3):
    xq = mxq(f64(xT)[:, unstriped(offs)], 0, "e4m3")
    y = mxq(f64(w1), 0, "e4m3").T @ xq
    e0 = np.exp(f64(score)[0, :1])
    e1 = np.exp(f64(score)[1, :1])
    e2 = np.exp(f64(score)[2, :1])
    num = y[:, unstriped(pos1)] * e0 + y[:, unstriped(pos2)] * e1 + y[:, unstriped(pos3)] * e2
    den = e0 + e1 + e2
    out_0 = num / den
    return (out_0,) + planes(out_0)

@@ -1,0 +1,204 @@
+from contextlib import ExitStack
+
+import concourse.mybir as mybir
+from concourse.masks import make_identity
+
+K, T, S, D, V, N = 512, 1024, 512, 3, 256, 512
+P = 128
+PACK = 4
+PER_COL = 16
+
+F32 = mybir.dt.float32
+BF16 = mybir.dt.bfloat16
+I32 = mybir.dt.int32
+U32 = mybir.dt.uint32
+U16 = mybir.dt.uint16
+U8 = mybir.dt.uint8
+FP8X4 = mybir.dt.float8_e4m3fn_x4
+ALU = mybir.AluOpType
+ACT = mybir.ActivationFunctionType
+AXIS = mybir.AxisListType
+
+FLOPS = 2 * K * N * S
+
+
+def entries(lst, a, b):
+    return lst[:, a // PER_COL : b // PER_COL]
+
+
+def tile_picked_gatv_none_lo_kernel(tc, xT, w1, score, offs, pos1, pos2, pos3, out_0, out_1, out_2):
+    nc = tc.nc
+    with ExitStack() as ctx:
+        lists = ctx.enter_context(tc.tile_pool(name="lists", bufs=1))
+        sb = ctx.enter_context(tc.tile_pool(name="sb", bufs=1))
+        ps = ctx.enter_context(tc.psum_pool(name="ps", bufs=1))
+
+        rows = sb.tile([P, D, P], F32, name="rows")
+        nc.vector.memset(rows[0 : P - 2, :, :], 0.0)
+        nc.scalar.dma_start(out=rows[P - 2 : P, :, :], in_=score[:, 0, :].rearrange("d (h p) -> h d p", h=2))
+        x_rows = xT.rearrange("(p j) n -> p j n", j=PACK)
+        xr = [sb.tile([P, T], F32, name=f"xr{j}") for j in range(PACK)]
+        idx = lists.tile([P, S // PER_COL], U16, name="idx")
+        nc.sync.dma_start(out=xr[0][:], in_=x_rows[:, 0, :])
+        nc.sync.dma_start(out=idx[:], in_=offs)
+        for j in range(1, PACK):
+            nc.sync.dma_start(out=xr[j][:], in_=x_rows[:, j, :])
+        w_rows = w1.rearrange("(p j) c -> p j c", j=PACK)
+        wr = sb.tile([P, PACK, N], F32, name="wr")
+        nc.sync.dma_start(out=wr[:], in_=w_rows)
+        pos = []
+        for d, src in enumerate((pos1, pos2, pos3)):
+            lst = lists.tile([P, V // PER_COL], U16, name=f"pos{d}")
+            nc.sync.dma_start(out=lst[:], in_=src)
+            pos.append(lst)
+
+        ident = sb.tile([P, P], F32, name="ident")
+        make_identity(nc, ident[:])
+        turned = ps.tile([P, D, P], F32, name="turned")
+        for d in range(D):
+            nc.tensor.transpose(turned[:, d, :], rows[:, d, :], ident[:])
+        sc = turned[:, :, P - 2 : P]
+        xg = sb.tile([P, PACK, S], F32, name="xg")
+        top = xg[:, 1, 0:2]
+        sh = xg[:, 2:4, 256:448:64].rearrange("p e d -> p d e")
+        inv = xg[:, 3, 0:2]
+        nc.vector.tensor_reduce(out=top, in_=sc.rearrange("p d e -> p e d"), axis=AXIS.X, op=ALU.max)
+        nc.vector.tensor_tensor(out=sh, in0=sc, in1=top.unsqueeze(1).to_broadcast([P, D, 2]), op=ALU.subtract)
+        ex = sb.tile([P, D, 2], F32, name="ex")
+        nc.scalar.activation(out=ex[:], in_=sh, func=ACT.Exp)
+        den = sb.tile([P, 2], F32, name="den")
+        nc.vector.tensor_reduce(out=den[:], in_=ex[:].rearrange("p d e -> p e d"), axis=AXIS.X, op=ALU.add)
+        nc.vector.reciprocal(out=inv, in_=den[:])
+        att = sb.tile([P, D, 2], F32, name="att")
+        nc.vector.tensor_tensor(out=att[:], in0=ex[:], in1=inv.unsqueeze(1).to_broadcast([P, D, 2]), op=ALU.mult)
+
+        nc.scalar.activation(out=xg[:, 0, :], in_=xr[0][:].indirect(idx[:]), func=ACT.Copy)
+        nc.vector.tensor_copy(out=xg[:, 1, :], in_=xr[1][:].indirect(idx[:]))
+        nc.scalar.activation(out=xg[:, 2, :], in_=xr[2][:].indirect(idx[:]), func=ACT.Copy)
+
+        spreads = []
+        for d0, d1 in ((0, 2), (2, 3)):
+            spread = ps.tile([P, d1 - d0, V], F32, name=f"spread{d0}")
+            for d in range(d0, d1):
+                for e in range(2):
+                    nc.tensor.transpose(spread[:, d - d0, e * P : (e + 1) * P], att[:, d, e : e + 1].to_broadcast([P, P]), ident[:])
+            spreads.append((d0, d1, spread))
+        nc.vector.tensor_copy(out=xg[:, 3, 0:256], in_=xr[3][:].indirect(entries(idx, 0, 256)))
+        for s0 in (256, 384):
+            nc.scalar.activation(out=xg[:, 3, s0 : s0 + 128], in_=xr[3][:].indirect(entries(idx, s0, s0 + 128)), func=ACT.Copy)
+
+        xq = sb.tile([P, S], U32, name="xq", align_bytes=64)
+        xs = sb.tile([P, S], U8, name="xs", align_bytes=64)
+        xb = sb.tile([P, S, PACK], BF16, name="xb", align_bytes=64)
+
+        def weave_x(copy, s0, s1):
+            copy(out=xb[:, s0:s1, :].rearrange("p (c i) j -> p c j i", i=4),
+                 in_=xg[:, :, s0:s1].rearrange("p j (c i) -> p c j i", i=4))
+
+        def quant_x():
+            nc.vector.quantize_mx(out=xq[:].bitcast(FP8X4), scales=xs[:], in_=xb[:].rearrange("p s j -> p (s j)"))
+
+        wb = xb[:].rearrange("p (t m) j -> p t m j", t=PACK)
+        wq = sb.tile([P, N], U32, name="wq", align_bytes=64)
+        ws = sb.tile([P, N], U8, name="ws", align_bytes=64)
+
+        def deal_w(copy, t0, t1, m0, m1):
+            copy(
+                out=wb[:, t0:t1, m0:m1, :].rearrange("p t m j -> p m j t"),
+                in_=wr[:].rearrange("p j (m t) -> p m j t", t=PACK)[:, m0:m1, :, t0:t1])
+
+        def quant_w(t):
+            cols = slice(t * P, (t + 1) * P)
+            nc.vector.quantize_mx(out=wq[:, cols].bitcast(FP8X4), scales=ws[:, cols], in_=wb[:, t, :, :].rearrange("p m j -> p (m j)"))
+
+        y = [sb.tile([P, S], F32, name=f"y{t}") for t in range(PACK)]
+
+        def project(t):
+            cols = slice(t * P, (t + 1) * P)
+            width = S // 2 if t == 0 else S
+            for s0 in range(0, S, width):
+                acc = ps.tile([P, width], F32, name=f"acc{t}_{s0}")
+                nc.tensor.matmul_mx(out=acc[:], lhsT=wq[:, cols].bitcast(FP8X4), lhsT_scale=ws[:, cols],
+                                    rhs=xq[:, s0 : s0 + width].bitcast(FP8X4), rhs_scale=xs[:, s0 : s0 + width], start=True, stop=True)
+                nc.scalar.copy(out=y[t][:, s0 : s0 + width], in_=acc[:])
+
+        weave_x(nc.vector.tensor_copy, 0, 256)
+        weave_x(nc.vector.tensor_copy, 256, 384)
+        weave_x(nc.scalar.copy, 384, 512)
+        a = xg[:].rearrange("p j s -> p (j s)")[:, 0 : D * V].rearrange("p (d v) -> p d v", d=D)
+        for d0, d1, spread in spreads:
+            nc.scalar.copy(out=a[:, d0:d1, :], in_=spread[:])
+        quant_x()
+        deal_w(nc.vector.tensor_copy, 0, 2, 0, P)
+        deal_w(nc.scalar.copy, 2, 4, 0, P // 2)
+        deal_w(nc.vector.tensor_copy, 2, 4, P // 2, P)
+        for t in range(PACK):
+            quant_w(t)
+            project(t)
+
+        term = [sb.tile([P, D, V], F32, name=f"term{t}") for t in range(PACK)]
+        raw = [sb.tile([P, D, V], F32, name=f"raw{t}") for t in range(PACK)]
+        part = [sb.tile([P, V], F32, name=f"part{t}") for t in range(PACK)]
+        o = sb.tile([P, PACK, V], F32, name="o")
+        out_rows = out_0.rearrange("(p t) v -> p t v", t=PACK)
+
+        def fused(t, d):
+            nc.vector.tensor_tensor(out=term[t][:, d, :], in0=y[t][:].indirect(pos[d][:]), in1=a[:, d, :], op=ALU.mult)
+
+        def fetch(t, d, a0=0, a1=V):
+            nc.scalar.activation(out=raw[t][:, d, a0:a1], in_=y[t][:].indirect(entries(pos[d], a0, a1)), func=ACT.Copy)
+
+        def weigh(t, d0, d1, a0=0, a1=V):
+            nc.vector.tensor_tensor(out=term[t][:, d0:d1, a0:a1], in0=raw[t][:, d0:d1, a0:a1], in1=a[:, d0:d1, a0:a1], op=ALU.mult)
+
+        def add01(t, da=0, db=1):
+            nc.vector.tensor_tensor(out=part[t][:], in0=term[t][:, da, :], in1=term[t][:, db, :], op=ALU.add)
+
+        def add2(t, a0=0, a1=V, d=2):
+            nc.vector.tensor_tensor(out=o[:, t, a0:a1], in0=part[t][:, a0:a1], in1=term[t][:, d, a0:a1], op=ALU.add)
+            nc.sync.dma_start(out=out_rows[:, t, a0:a1], in_=o[:, t, a0:a1])
+
+        ob = [sb.tile([P, V // 2, PACK], BF16, name=f"ob{h}", align_bytes=64) for h in range(2)]
+        oq = sb.tile([P, V], U32, name="oq", align_bytes=64)
+        osc = sb.tile([P, V], U8, name="osc", align_bytes=64)
+        words_out = out_1[0].rearrange("p c r -> p (c r)").bitcast(I32)
+
+        def round_o(copy, h):
+            copy(out=ob[h][:].rearrange("p (c i) t -> p c t i", i=4),
+                 in_=o[:, :, h * (V // 2) : (h + 1) * (V // 2)].rearrange("p t (c i) -> p c t i", i=4))
+
+        def quant_o(h):
+            cols = slice(h * (V // 2), (h + 1) * (V // 2))
+            nc.vector.quantize_mx(out=oq[:, cols].bitcast(FP8X4), scales=osc[:, cols], in_=ob[h][:].rearrange("p v t -> p (v t)"))
+            nc.sync.dma_start(out=words_out[:, cols], in_=oq[:, cols].bitcast(I32))
+
+        H = V // 2
+        for t, d in ((1, 0), (1, 1), (1, 2), (2, 0), (2, 1), (2, 2), (3, 0)):
+            fetch(t, d)
+        fused(0, 0)
+        fused(0, 1)
+        fused(0, 2)
+        add01(0)
+        fused(3, 1)
+        add2(0)
+        weigh(1, 0, 2)
+        fused(3, 2)
+        add01(1)
+        weigh(1, 2, 3)
+        add01(3, 1, 2)
+        add2(1)
+        weigh(2, 0, 2)
+        weigh(2, 2, 3)
+        add01(2)
+        weigh(3, 0, 1)
+        add2(2, 0, H)
+        add2(3, 0, H, 0)
+        add2(2, H, V)
+        add2(3, H, V, 0)
+        round_o(nc.scalar.copy, 0)
+        round_o(nc.vector.tensor_copy, 1)
+        quant_o(0)
+        quant_o(1)
+        for q in range(4):
+            eng = nc.sync if q < 2 else nc.scalar
+            eng.dma_start(out=out_2[0, 4 * q : 4 * q + 4, :].bitcast(I32), in_=osc[32 * q : 32 * q + 4, :].bitcast(I32))

@@ -6,7 +6,13 @@ from concourse.masks import make_identity
 K, T, S, D, V, N = 512, 1024, 512, 3, 256, 512
 P = 128
 PACK = 4
-PER_COL = 16
+PER_COLUMN = 16
+QUARTER = S // 4
+HALF_S = S // 2
+HALF_V = V // 2
+HALVES = V // P
+WEAVE_SPLIT = 448
+DEAL_SPLIT = 88
 
 F32 = mybir.dt.float32
 BF16 = mybir.dt.bfloat16
@@ -22,8 +28,8 @@ AXIS = mybir.AxisListType
 FLOPS = 2 * K * N * S
 
 
-def entries(lst, a, b):
-    return lst[:, a // PER_COL : b // PER_COL]
+def entries(lst, start, stop):
+    return lst[:, start // PER_COLUMN : stop // PER_COLUMN]
 
 
 def tile_picked_gatv_none_lo_kernel(tc, xT, w1, score, offs, pos1, pos2, pos3, out_0, out_1, out_2):
@@ -33,22 +39,24 @@ def tile_picked_gatv_none_lo_kernel(tc, xT, w1, score, offs, pos1, pos2, pos3, o
         sb = ctx.enter_context(tc.tile_pool(name="sb", bufs=1))
         ps = ctx.enter_context(tc.psum_pool(name="ps", bufs=1))
 
-        rows = sb.tile([P, D, P], F32, name="rows")
-        nc.vector.memset(rows[0 : P - 2, :, :], 0.0)
-        nc.scalar.dma_start(out=rows[P - 2 : P, :, :], in_=score[:, 0, :].rearrange("d (h p) -> h d p", h=2))
+        score_rows = sb.tile([P, D, P], F32, name="score_rows")
+        nc.vector.memset(score_rows[0 : P - HALVES, :, :], 0.0)
+        nc.scalar.dma_start(out=score_rows[P - HALVES : P, :, :], in_=score[:, 0, :].rearrange("d (h p) -> h d p", h=HALVES))
+        warm = sb.tile([P, 2], F32, name="warm")
+        nc.vector.memset(warm[:, 0:1], 0.0)
+        nc.scalar.activation(out=warm[:, 1:2], in_=warm[:, 0:1], func=ACT.Exp)
         x_rows = xT.rearrange("(p j) n -> p j n", j=PACK)
-        xr = [sb.tile([P, T], F32, name=f"xr{j}") for j in range(PACK)]
-        idx = lists.tile([P, S // PER_COL], U16, name="idx")
-        nc.sync.dma_start(out=xr[0][:], in_=x_rows[:, 0, :])
+        x_plane = [sb.tile([P, T], F32, name=f"x_plane{j}") for j in range(PACK)]
+        idx = lists.tile([P, S // PER_COLUMN], U16, name="idx")
+        nc.sync.dma_start(out=x_plane[0][:], in_=x_rows[:, 0, :])
         nc.sync.dma_start(out=idx[:], in_=offs)
         for j in range(1, PACK):
-            nc.sync.dma_start(out=xr[j][:], in_=x_rows[:, j, :])
-        w_rows = w1.rearrange("(p j) c -> p j c", j=PACK)
-        wr = sb.tile([P, PACK, N], F32, name="wr")
-        nc.sync.dma_start(out=wr[:], in_=w_rows)
+            nc.sync.dma_start(out=x_plane[j][:], in_=x_rows[:, j, :])
+        w_raw = sb.tile([P, PACK, N], F32, name="w_raw")
+        nc.sync.dma_start(out=w_raw[:], in_=w1.rearrange("(p j) m -> p j m", j=PACK))
         pos = []
         for d, src in enumerate((pos1, pos2, pos3)):
-            lst = lists.tile([P, V // PER_COL], U16, name=f"pos{d}")
+            lst = lists.tile([P, V // PER_COLUMN], U16, name=f"pos{d}")
             nc.sync.dma_start(out=lst[:], in_=src)
             pos.append(lst)
 
@@ -56,149 +64,170 @@ def tile_picked_gatv_none_lo_kernel(tc, xT, w1, score, offs, pos1, pos2, pos3, o
         make_identity(nc, ident[:])
         turned = ps.tile([P, D, P], F32, name="turned")
         for d in range(D):
-            nc.tensor.transpose(turned[:, d, :], rows[:, d, :], ident[:])
-        sc = turned[:, :, P - 2 : P]
-        xg = sb.tile([P, PACK, S], F32, name="xg")
-        top = xg[:, 1, 0:2]
-        sh = xg[:, 2:4, 256:448:64].rearrange("p e d -> p d e")
-        inv = xg[:, 3, 0:2]
-        nc.vector.tensor_reduce(out=top, in_=sc.rearrange("p d e -> p e d"), axis=AXIS.X, op=ALU.max)
-        nc.vector.tensor_tensor(out=sh, in0=sc, in1=top.unsqueeze(1).to_broadcast([P, D, 2]), op=ALU.subtract)
-        ex = sb.tile([P, D, 2], F32, name="ex")
-        nc.scalar.activation(out=ex[:], in_=sh, func=ACT.Exp)
-        den = sb.tile([P, 2], F32, name="den")
-        nc.vector.tensor_reduce(out=den[:], in_=ex[:].rearrange("p d e -> p e d"), axis=AXIS.X, op=ALU.add)
-        nc.vector.reciprocal(out=inv, in_=den[:])
-        att = sb.tile([P, D, 2], F32, name="att")
-        nc.vector.tensor_tensor(out=att[:], in0=ex[:], in1=inv.unsqueeze(1).to_broadcast([P, D, 2]), op=ALU.mult)
+            nc.tensor.transpose(turned[:, d, :], score_rows[:, d, :], ident[:])
+        s_cols = turned[:, :, P - HALVES : P]
 
-        nc.scalar.activation(out=xg[:, 0, :], in_=xr[0][:].indirect(idx[:]), func=ACT.Copy)
-        nc.vector.tensor_copy(out=xg[:, 1, :], in_=xr[1][:].indirect(idx[:]))
-        nc.scalar.activation(out=xg[:, 2, :], in_=xr[2][:].indirect(idx[:]), func=ACT.Copy)
+        picked = sb.tile([P, PACK, S], F32, name="picked")
+        picked_flat = picked[:].rearrange("p j s -> p (j s)")
+        neg_top = picked_flat[:, 2 * S - 1 : 2 * S + 1]
+        den = picked[:, 3, 3 * QUARTER - 1 : 3 * QUARTER + 1]
+        inv_den = picked[:, 3, QUARTER - 1 : QUARTER + 1]
+        expd = sb.tile([P, D, HALVES], F32, name="expd")
+        att = sb.tile([P, D, HALVES], F32, name="att")
+        nc.vector.tensor_reduce(out=neg_top, in_=s_cols.rearrange("p d h -> p h d"), axis=AXIS.X, op=ALU.max, negate=True)
+        for h in range(HALVES):
+            nc.scalar.activation(
+                out=expd[:, :, h], in_=s_cols[:, :, h], func=ACT.Exp, bias=neg_top[:, h : h + 1], accum_out=den[:, h : h + 1]
+            )
+        nc.vector.reciprocal(out=inv_den, in_=den)
+        nc.vector.tensor_tensor(out=att[:], in0=expd[:], in1=inv_den.unsqueeze(1).to_broadcast([P, D, HALVES]), op=ALU.mult)
 
         spreads = []
-        for d0, d1 in ((0, 2), (2, 3)):
+        for d0, d1 in ((0, 2), (2, D)):
             spread = ps.tile([P, d1 - d0, V], F32, name=f"spread{d0}")
             for d in range(d0, d1):
-                for e in range(2):
-                    nc.tensor.transpose(spread[:, d - d0, e * P : (e + 1) * P], att[:, d, e : e + 1].to_broadcast([P, P]), ident[:])
+                for h in range(HALVES):
+                    nc.tensor.transpose(spread[:, d - d0, h * P : (h + 1) * P], att[:, d, h : h + 1].to_broadcast([P, P]), ident[:])
             spreads.append((d0, d1, spread))
-        nc.vector.tensor_copy(out=xg[:, 3, 0:256], in_=xr[3][:].indirect(entries(idx, 0, 256)))
-        for s0 in (256, 384):
-            nc.scalar.activation(out=xg[:, 3, s0 : s0 + 128], in_=xr[3][:].indirect(entries(idx, s0, s0 + 128)), func=ACT.Copy)
 
-        xq = sb.tile([P, S], U32, name="xq", align_bytes=64)
-        xs = sb.tile([P, S], U8, name="xs", align_bytes=64)
-        xb = sb.tile([P, S, PACK], BF16, name="xb", align_bytes=64)
+        def pick_on_vector(j, s0, s1):
+            nc.vector.tensor_copy(out=picked[:, j, s0:s1], in_=x_plane[j][:].indirect(entries(idx, s0, s1)))
+
+        def pick_on_scalar(j, s0, s1):
+            nc.scalar.activation(out=picked[:, j, s0:s1], in_=x_plane[j][:].indirect(entries(idx, s0, s1)), func=ACT.Copy)
+
+        pick_on_scalar(0, 0, S)
+        pick_on_vector(1, 0, S)
+        pick_on_scalar(2, 0, S)
+        for s0 in range(0, HALF_S, QUARTER):
+            pick_on_vector(3, s0, s0 + QUARTER)
+        for s0 in range(HALF_S, S, QUARTER):
+            pick_on_scalar(3, s0, s0 + QUARTER)
+
+        woven = sb.tile([P, S, PACK], BF16, name="woven", align_bytes=64)
 
         def weave_x(copy, s0, s1):
-            copy(out=xb[:, s0:s1, :].rearrange("p (c i) j -> p c j i", i=4),
-                 in_=xg[:, :, s0:s1].rearrange("p j (c i) -> p c j i", i=4))
-
-        def quant_x():
-            nc.vector.quantize_mx(out=xq[:].bitcast(FP8X4), scales=xs[:], in_=xb[:].rearrange("p s j -> p (s j)"))
-
-        wb = xb[:].rearrange("p (t m) j -> p t m j", t=PACK)
-        wq = sb.tile([P, N], U32, name="wq", align_bytes=64)
-        ws = sb.tile([P, N], U8, name="ws", align_bytes=64)
-
-        def deal_w(copy, t0, t1, m0, m1):
             copy(
-                out=wb[:, t0:t1, m0:m1, :].rearrange("p t m j -> p m j t"),
-                in_=wr[:].rearrange("p j (m t) -> p m j t", t=PACK)[:, m0:m1, :, t0:t1])
+                out=woven[:, s0:s1, :].rearrange("p (c i) j -> p c j i", i=4),
+                in_=picked[:, :, s0:s1].rearrange("p j (c i) -> p c j i", i=4),
+            )
 
-        def quant_w(t):
-            cols = slice(t * P, (t + 1) * P)
-            nc.vector.quantize_mx(out=wq[:, cols].bitcast(FP8X4), scales=ws[:, cols], in_=wb[:, t, :, :].rearrange("p m j -> p (m j)"))
+        weave_x(nc.vector.tensor_copy, 0, QUARTER)
+        weave_x(nc.vector.tensor_copy, QUARTER, HALF_S)
+        weave_x(nc.vector.tensor_copy, HALF_S, WEAVE_SPLIT)
+        weave_x(nc.scalar.copy, WEAVE_SPLIT, S)
 
-        y = [sb.tile([P, S], F32, name=f"y{t}") for t in range(PACK)]
-
-        def project(t):
-            cols = slice(t * P, (t + 1) * P)
-            width = S // 2 if t == 0 else S
-            for s0 in range(0, S, width):
-                acc = ps.tile([P, width], F32, name=f"acc{t}_{s0}")
-                nc.tensor.matmul_mx(out=acc[:], lhsT=wq[:, cols].bitcast(FP8X4), lhsT_scale=ws[:, cols],
-                                    rhs=xq[:, s0 : s0 + width].bitcast(FP8X4), rhs_scale=xs[:, s0 : s0 + width], start=True, stop=True)
-                nc.scalar.copy(out=y[t][:, s0 : s0 + width], in_=acc[:])
-
-        weave_x(nc.vector.tensor_copy, 0, 256)
-        weave_x(nc.vector.tensor_copy, 256, 384)
-        weave_x(nc.scalar.copy, 384, 512)
-        a = xg[:].rearrange("p j s -> p (j s)")[:, 0 : D * V].rearrange("p (d v) -> p d v", d=D)
+        a = picked_flat[:, 0 : D * V].rearrange("p (d v) -> p d v", d=D)
         for d0, d1, spread in spreads:
             nc.scalar.copy(out=a[:, d0:d1, :], in_=spread[:])
-        quant_x()
-        deal_w(nc.vector.tensor_copy, 0, 2, 0, P)
-        deal_w(nc.scalar.copy, 2, 4, 0, P // 2)
-        deal_w(nc.vector.tensor_copy, 2, 4, P // 2, P)
-        for t in range(PACK):
-            quant_w(t)
-            project(t)
 
+        x_words = sb.tile([P, S], U32, name="x_words", align_bytes=64)
+        x_scales = sb.tile([P, S], U8, name="x_scales", align_bytes=64)
+        for s0 in range(0, S, HALF_S):
+            cols = slice(s0, s0 + HALF_S)
+            nc.vector.quantize_mx(
+                out=x_words[:, cols].bitcast(FP8X4), scales=x_scales[:, cols], in_=woven[:, cols, :].rearrange("p s j -> p (s j)")
+            )
+
+        dealt = woven[:].rearrange("p (t r) j -> p t r j", t=PACK)
+
+        def deal_w(copy, t0, t1, r0, r1):
+            copy(
+                out=dealt[:, t0:t1, r0:r1, :].rearrange("p t r j -> p r j t"),
+                in_=w_raw[:].rearrange("p j (r t) -> p r j t", t=PACK)[:, r0:r1, :, t0:t1],
+            )
+
+        deal_w(nc.vector.tensor_copy, 0, 2, 0, DEAL_SPLIT)
+        deal_w(nc.scalar.copy, 0, 2, DEAL_SPLIT, P)
+        deal_w(nc.scalar.copy, 2, PACK, 0, P // 2)
+        deal_w(nc.vector.tensor_copy, 2, PACK, P // 2, P)
+
+        w_words = sb.tile([P, N], U32, name="w_words", align_bytes=64)
+        w_scales = sb.tile([P, N], U8, name="w_scales", align_bytes=64)
+        y = [sb.tile([P, S], F32, name=f"y{t}") for t in range(PACK)]
+        for t in range(PACK):
+            rows = slice(t * P, (t + 1) * P)
+            nc.vector.quantize_mx(
+                out=w_words[:, rows].bitcast(FP8X4), scales=w_scales[:, rows], in_=dealt[:, t, :, :].rearrange("p r j -> p (r j)")
+            )
+            width = HALF_S if t == 0 else S
+            for s0 in range(0, S, width):
+                cols = slice(s0, s0 + width)
+                acc = ps.tile([P, width], F32, name=f"acc{t}_{s0}")
+                nc.tensor.matmul_mx(
+                    out=acc[:],
+                    lhsT=w_words[:, rows].bitcast(FP8X4),
+                    lhsT_scale=w_scales[:, rows],
+                    rhs=x_words[:, cols].bitcast(FP8X4),
+                    rhs_scale=x_scales[:, cols],
+                    start=True,
+                    stop=True,
+                )
+                nc.scalar.copy(out=y[t][:, cols], in_=acc[:])
+
+        fetched = [sb.tile([P, D, V], F32, name=f"fetched{t}") for t in range(PACK)]
         term = [sb.tile([P, D, V], F32, name=f"term{t}") for t in range(PACK)]
-        raw = [sb.tile([P, D, V], F32, name=f"raw{t}") for t in range(PACK)]
         part = [sb.tile([P, V], F32, name=f"part{t}") for t in range(PACK)]
-        o = sb.tile([P, PACK, V], F32, name="o")
+        res = sb.tile([P, PACK, V], F32, name="res")
         out_rows = out_0.rearrange("(p t) v -> p t v", t=PACK)
 
-        def fused(t, d):
+        def fetch(t, d):
+            nc.scalar.activation(out=fetched[t][:, d, :], in_=y[t][:].indirect(pos[d][:]), func=ACT.Copy)
+
+        def weigh(t, d0, d1):
+            nc.vector.tensor_tensor(out=term[t][:, d0:d1, :], in0=fetched[t][:, d0:d1, :], in1=a[:, d0:d1, :], op=ALU.mult)
+
+        def fetch_and_weigh(t, d):
             nc.vector.tensor_tensor(out=term[t][:, d, :], in0=y[t][:].indirect(pos[d][:]), in1=a[:, d, :], op=ALU.mult)
 
-        def fetch(t, d, a0=0, a1=V):
-            nc.scalar.activation(out=raw[t][:, d, a0:a1], in_=y[t][:].indirect(entries(pos[d], a0, a1)), func=ACT.Copy)
+        def add_first_two(t):
+            nc.vector.tensor_tensor(out=part[t][:], in0=term[t][:, 0, :], in1=term[t][:, 1, :], op=ALU.add)
 
-        def weigh(t, d0, d1, a0=0, a1=V):
-            nc.vector.tensor_tensor(out=term[t][:, d0:d1, a0:a1], in0=raw[t][:, d0:d1, a0:a1], in1=a[:, d0:d1, a0:a1], op=ALU.mult)
+        def add_third(t, v0=0, v1=V):
+            nc.vector.tensor_tensor(out=res[:, t, v0:v1], in0=part[t][:, v0:v1], in1=term[t][:, 2, v0:v1], op=ALU.add)
 
-        def add01(t, da=0, db=1):
-            nc.vector.tensor_tensor(out=part[t][:], in0=term[t][:, da, :], in1=term[t][:, db, :], op=ALU.add)
+        def store(t):
+            nc.sync.dma_start(out=out_rows[:, t, :], in_=res[:, t, :])
 
-        def add2(t, a0=0, a1=V, d=2):
-            nc.vector.tensor_tensor(out=o[:, t, a0:a1], in0=part[t][:, a0:a1], in1=term[t][:, d, a0:a1], op=ALU.add)
-            nc.sync.dma_start(out=out_rows[:, t, a0:a1], in_=o[:, t, a0:a1])
-
-        ob = [sb.tile([P, V // 2, PACK], BF16, name=f"ob{h}", align_bytes=64) for h in range(2)]
-        oq = sb.tile([P, V], U32, name="oq", align_bytes=64)
-        osc = sb.tile([P, V], U8, name="osc", align_bytes=64)
-        words_out = out_1[0].rearrange("p c r -> p (c r)").bitcast(I32)
-
-        def round_o(copy, h):
-            copy(out=ob[h][:].rearrange("p (c i) t -> p c t i", i=4),
-                 in_=o[:, :, h * (V // 2) : (h + 1) * (V // 2)].rearrange("p t (c i) -> p c t i", i=4))
-
-        def quant_o(h):
-            cols = slice(h * (V // 2), (h + 1) * (V // 2))
-            nc.vector.quantize_mx(out=oq[:, cols].bitcast(FP8X4), scales=osc[:, cols], in_=ob[h][:].rearrange("p v t -> p (v t)"))
-            nc.sync.dma_start(out=words_out[:, cols], in_=oq[:, cols].bitcast(I32))
-
-        H = V // 2
-        for t, d in ((1, 0), (1, 1), (1, 2), (2, 0), (2, 1), (2, 2), (3, 0)):
+        for t, d in ((1, 0), (1, 1), (1, 2), (2, 0), (2, 1), (3, 2), (2, 2)):
             fetch(t, d)
-        fused(0, 0)
-        fused(0, 1)
-        fused(0, 2)
-        add01(0)
-        fused(3, 1)
-        add2(0)
+        for d in range(D):
+            fetch_and_weigh(0, d)
+        add_first_two(0)
+        fetch_and_weigh(3, 0)
+        add_third(0)
+        store(0)
         weigh(1, 0, 2)
-        fused(3, 2)
-        add01(1)
-        weigh(1, 2, 3)
-        add01(3, 1, 2)
-        add2(1)
+        fetch_and_weigh(3, 1)
+        add_first_two(1)
+        weigh(1, 2, D)
+        add_first_two(3)
+        add_third(1)
+        store(1)
         weigh(2, 0, 2)
-        weigh(2, 2, 3)
-        add01(2)
-        weigh(3, 0, 1)
-        add2(2, 0, H)
-        add2(3, 0, H, 0)
-        add2(2, H, V)
-        add2(3, H, V, 0)
-        round_o(nc.scalar.copy, 0)
-        round_o(nc.vector.tensor_copy, 1)
-        quant_o(0)
-        quant_o(1)
+        weigh(3, 2, D)
+        add_first_two(2)
+        weigh(2, 2, D)
+        add_third(3)
+        store(3)
+        add_third(2, 0, HALF_V)
+        add_third(2, HALF_V, V)
+        store(2)
+
+        rounded = sb.tile([P, V, PACK], BF16, name="rounded", align_bytes=64)
+        o_words = sb.tile([P, V], U32, name="o_words", align_bytes=64)
+        o_scales = sb.tile([P, V], U8, name="o_scales", align_bytes=64)
+        for v0 in range(0, V, HALF_V):
+            nc.vector.tensor_copy(
+                out=rounded[:, v0 : v0 + HALF_V, :].rearrange("p (c i) t -> p c t i", i=4),
+                in_=res[:, :, v0 : v0 + HALF_V].rearrange("p t (c i) -> p c t i", i=4),
+            )
+        for v0 in range(0, V, HALF_V):
+            cols = slice(v0, v0 + HALF_V)
+            nc.vector.quantize_mx(
+                out=o_words[:, cols].bitcast(FP8X4), scales=o_scales[:, cols], in_=rounded[:, cols, :].rearrange("p v t -> p (v t)")
+            )
+        nc.sync.dma_start(out=out_1[0].rearrange("p v t -> p (v t)").bitcast(I32), in_=o_words[:].bitcast(I32))
         for q in range(4):
-            eng = nc.sync if q < 2 else nc.scalar
-            eng.dma_start(out=out_2[0, 4 * q : 4 * q + 4, :].bitcast(I32), in_=osc[32 * q : 32 * q + 4, :].bitcast(I32))
+            queue = nc.sync if q < 2 else nc.scalar
+            queue.dma_start(out=out_2[0, 4 * q : 4 * q + 4, :].bitcast(I32), in_=o_scales[32 * q : 32 * q + 4, :].bitcast(I32))

from contextlib import ExitStack

import concourse.mybir as mybir
from concourse.masks import make_identity

K, T, S, D, V, N = 512, 1024, 512, 3, 256, 512
P = 128
PACK = 4
PER_COLUMN = 16
QUARTER = S // 4
HALF_S = S // 2
HALF_V = V // 2
HALVES = V // P
WEAVE_SPLIT = 448
DEAL_SPLIT = 88

F32 = mybir.dt.float32
BF16 = mybir.dt.bfloat16
I32 = mybir.dt.int32
U32 = mybir.dt.uint32
U16 = mybir.dt.uint16
U8 = mybir.dt.uint8
FP8X4 = mybir.dt.float8_e4m3fn_x4
ALU = mybir.AluOpType
ACT = mybir.ActivationFunctionType
AXIS = mybir.AxisListType

FLOPS = 2 * K * N * S


def entries(lst, start, stop):
    return lst[:, start // PER_COLUMN : stop // PER_COLUMN]


def tile_picked_gatv_none_lo_kernel(tc, xT, w1, score, offs, pos1, pos2, pos3, out_0, out_1, out_2):
    nc = tc.nc
    with ExitStack() as ctx:
        lists = ctx.enter_context(tc.tile_pool(name="lists", bufs=1))
        sb = ctx.enter_context(tc.tile_pool(name="sb", bufs=1))
        ps = ctx.enter_context(tc.psum_pool(name="ps", bufs=1))

        score_rows = sb.tile([P, D, P], F32, name="score_rows")
        nc.vector.memset(score_rows[0 : P - HALVES, :, :], 0.0)
        nc.scalar.dma_start(out=score_rows[P - HALVES : P, :, :], in_=score[:, 0, :].rearrange("d (h p) -> h d p", h=HALVES))
        warm = sb.tile([P, 2], F32, name="warm")
        nc.vector.memset(warm[:, 0:1], 0.0)
        nc.scalar.activation(out=warm[:, 1:2], in_=warm[:, 0:1], func=ACT.Exp)
        x_rows = xT.rearrange("(p j) n -> p j n", j=PACK)
        x_plane = [sb.tile([P, T], F32, name=f"x_plane{j}") for j in range(PACK)]
        idx = lists.tile([P, S // PER_COLUMN], U16, name="idx")
        nc.sync.dma_start(out=x_plane[0][:], in_=x_rows[:, 0, :])
        nc.sync.dma_start(out=idx[:], in_=offs)
        for j in range(1, PACK):
            nc.sync.dma_start(out=x_plane[j][:], in_=x_rows[:, j, :])
        w_raw = sb.tile([P, PACK, N], F32, name="w_raw")
        nc.sync.dma_start(out=w_raw[:], in_=w1.rearrange("(p j) m -> p j m", j=PACK))
        pos = []
        for d, src in enumerate((pos1, pos2, pos3)):
            lst = lists.tile([P, V // PER_COLUMN], U16, name=f"pos{d}")
            nc.sync.dma_start(out=lst[:], in_=src)
            pos.append(lst)

        ident = sb.tile([P, P], F32, name="ident")
        make_identity(nc, ident[:])
        turned = ps.tile([P, D, P], F32, name="turned")
        for d in range(D):
            nc.tensor.transpose(turned[:, d, :], score_rows[:, d, :], ident[:])
        s_cols = turned[:, :, P - HALVES : P]

        picked = sb.tile([P, PACK, S], F32, name="picked")
        picked_flat = picked[:].rearrange("p j s -> p (j s)")
        neg_top = picked_flat[:, 2 * S - 1 : 2 * S + 1]
        den = picked[:, 3, 3 * QUARTER - 1 : 3 * QUARTER + 1]
        inv_den = picked[:, 3, QUARTER - 1 : QUARTER + 1]
        expd = sb.tile([P, D, HALVES], F32, name="expd")
        att = sb.tile([P, D, HALVES], F32, name="att")
        nc.vector.tensor_reduce(out=neg_top, in_=s_cols.rearrange("p d h -> p h d"), axis=AXIS.X, op=ALU.max, negate=True)
        for h in range(HALVES):
            nc.scalar.activation(
                out=expd[:, :, h], in_=s_cols[:, :, h], func=ACT.Exp, bias=neg_top[:, h : h + 1], accum_out=den[:, h : h + 1]
            )
        nc.vector.reciprocal(out=inv_den, in_=den)
        nc.vector.tensor_tensor(out=att[:], in0=expd[:], in1=inv_den.unsqueeze(1).to_broadcast([P, D, HALVES]), op=ALU.mult)

        spreads = []
        for d0, d1 in ((0, 2), (2, D)):
            spread = ps.tile([P, d1 - d0, V], F32, name=f"spread{d0}")
            for d in range(d0, d1):
                for h in range(HALVES):
                    nc.tensor.transpose(spread[:, d - d0, h * P : (h + 1) * P], att[:, d, h : h + 1].to_broadcast([P, P]), ident[:])
            spreads.append((d0, d1, spread))

        def pick_on_vector(j, s0, s1):
            nc.vector.tensor_copy(out=picked[:, j, s0:s1], in_=x_plane[j][:].indirect(entries(idx, s0, s1)))

        def pick_on_scalar(j, s0, s1):
            nc.scalar.activation(out=picked[:, j, s0:s1], in_=x_plane[j][:].indirect(entries(idx, s0, s1)), func=ACT.Copy)

        pick_on_scalar(0, 0, S)
        pick_on_vector(1, 0, S)
        pick_on_scalar(2, 0, S)
        for s0 in range(0, HALF_S, QUARTER):
            pick_on_vector(3, s0, s0 + QUARTER)
        for s0 in range(HALF_S, S, QUARTER):
            pick_on_scalar(3, s0, s0 + QUARTER)

        woven = sb.tile([P, S, PACK], BF16, name="woven", align_bytes=64)

        def weave_x(copy, s0, s1):
            copy(
                out=woven[:, s0:s1, :].rearrange("p (c i) j -> p c j i", i=4),
                in_=picked[:, :, s0:s1].rearrange("p j (c i) -> p c j i", i=4),
            )

        weave_x(nc.vector.tensor_copy, 0, QUARTER)
        weave_x(nc.vector.tensor_copy, QUARTER, HALF_S)
        weave_x(nc.vector.tensor_copy, HALF_S, WEAVE_SPLIT)
        weave_x(nc.scalar.copy, WEAVE_SPLIT, S)

        a = picked_flat[:, 0 : D * V].rearrange("p (d v) -> p d v", d=D)
        for d0, d1, spread in spreads:
            nc.scalar.copy(out=a[:, d0:d1, :], in_=spread[:])

        x_words = sb.tile([P, S], U32, name="x_words", align_bytes=64)
        x_scales = sb.tile([P, S], U8, name="x_scales", align_bytes=64)
        for s0 in range(0, S, HALF_S):
            cols = slice(s0, s0 + HALF_S)
            nc.vector.quantize_mx(
                out=x_words[:, cols].bitcast(FP8X4), scales=x_scales[:, cols], in_=woven[:, cols, :].rearrange("p s j -> p (s j)")
            )

        dealt = woven[:].rearrange("p (t r) j -> p t r j", t=PACK)

        def deal_w(copy, t0, t1, r0, r1):
            copy(
                out=dealt[:, t0:t1, r0:r1, :].rearrange("p t r j -> p r j t"),
                in_=w_raw[:].rearrange("p j (r t) -> p r j t", t=PACK)[:, r0:r1, :, t0:t1],
            )

        deal_w(nc.vector.tensor_copy, 0, 2, 0, DEAL_SPLIT)
        deal_w(nc.scalar.copy, 0, 2, DEAL_SPLIT, P)
        deal_w(nc.scalar.copy, 2, PACK, 0, P // 2)
        deal_w(nc.vector.tensor_copy, 2, PACK, P // 2, P)

        w_words = sb.tile([P, N], U32, name="w_words", align_bytes=64)
        w_scales = sb.tile([P, N], U8, name="w_scales", align_bytes=64)
        y = [sb.tile([P, S], F32, name=f"y{t}") for t in range(PACK)]
        for t in range(PACK):
            rows = slice(t * P, (t + 1) * P)
            nc.vector.quantize_mx(
                out=w_words[:, rows].bitcast(FP8X4), scales=w_scales[:, rows], in_=dealt[:, t, :, :].rearrange("p r j -> p (r j)")
            )
            width = HALF_S if t == 0 else S
            for s0 in range(0, S, width):
                cols = slice(s0, s0 + width)
                acc = ps.tile([P, width], F32, name=f"acc{t}_{s0}")
                nc.tensor.matmul_mx(
                    out=acc[:],
                    lhsT=w_words[:, rows].bitcast(FP8X4),
                    lhsT_scale=w_scales[:, rows],
                    rhs=x_words[:, cols].bitcast(FP8X4),
                    rhs_scale=x_scales[:, cols],
                    start=True,
                    stop=True,
                )
                nc.scalar.copy(out=y[t][:, cols], in_=acc[:])

        fetched = [sb.tile([P, D, V], F32, name=f"fetched{t}") for t in range(PACK)]
        term = [sb.tile([P, D, V], F32, name=f"term{t}") for t in range(PACK)]
        part = [sb.tile([P, V], F32, name=f"part{t}") for t in range(PACK)]
        res = sb.tile([P, PACK, V], F32, name="res")
        out_rows = out_0.rearrange("(p t) v -> p t v", t=PACK)

        def fetch(t, d):
            nc.scalar.activation(out=fetched[t][:, d, :], in_=y[t][:].indirect(pos[d][:]), func=ACT.Copy)

        def weigh(t, d0, d1):
            nc.vector.tensor_tensor(out=term[t][:, d0:d1, :], in0=fetched[t][:, d0:d1, :], in1=a[:, d0:d1, :], op=ALU.mult)

        def fetch_and_weigh(t, d):
            nc.vector.tensor_tensor(out=term[t][:, d, :], in0=y[t][:].indirect(pos[d][:]), in1=a[:, d, :], op=ALU.mult)

        def add_first_two(t):
            nc.vector.tensor_tensor(out=part[t][:], in0=term[t][:, 0, :], in1=term[t][:, 1, :], op=ALU.add)

        def add_third(t, v0=0, v1=V):
            nc.vector.tensor_tensor(out=res[:, t, v0:v1], in0=part[t][:, v0:v1], in1=term[t][:, 2, v0:v1], op=ALU.add)

        def store(t):
            nc.sync.dma_start(out=out_rows[:, t, :], in_=res[:, t, :])

        for t, d in ((1, 0), (1, 1), (1, 2), (2, 0), (2, 1), (3, 2), (2, 2)):
            fetch(t, d)
        for d in range(D):
            fetch_and_weigh(0, d)
        add_first_two(0)
        fetch_and_weigh(3, 0)
        add_third(0)
        store(0)
        weigh(1, 0, 2)
        fetch_and_weigh(3, 1)
        add_first_two(1)
        weigh(1, 2, D)
        add_first_two(3)
        add_third(1)
        store(1)
        weigh(2, 0, 2)
        weigh(3, 2, D)
        add_first_two(2)
        weigh(2, 2, D)
        add_third(3)
        store(3)
        add_third(2, 0, HALF_V)
        add_third(2, HALF_V, V)
        store(2)

        rounded = sb.tile([P, V, PACK], BF16, name="rounded", align_bytes=64)
        o_words = sb.tile([P, V], U32, name="o_words", align_bytes=64)
        o_scales = sb.tile([P, V], U8, name="o_scales", align_bytes=64)
        for v0 in range(0, V, HALF_V):
            nc.vector.tensor_copy(
                out=rounded[:, v0 : v0 + HALF_V, :].rearrange("p (c i) t -> p c t i", i=4),
                in_=res[:, :, v0 : v0 + HALF_V].rearrange("p t (c i) -> p c t i", i=4),
            )
        for v0 in range(0, V, HALF_V):
            cols = slice(v0, v0 + HALF_V)
            nc.vector.quantize_mx(
                out=o_words[:, cols].bitcast(FP8X4), scales=o_scales[:, cols], in_=rounded[:, cols, :].rearrange("p v t -> p (v t)")
            )
        nc.sync.dma_start(out=out_1[0].rearrange("p v t -> p (v t)").bitcast(I32), in_=o_words[:].bitcast(I32))
        for q in range(4):
            queue = nc.sync if q < 2 else nc.scalar
            queue.dma_start(out=out_2[0, 4 * q : 4 * q + 4, :].bitcast(I32), in_=o_scales[32 * q : 32 * q + 4, :].bitcast(I32))
